import numpy as np
import ml_dtypes


def mxq(x, axis, fmt="e4m3"):
    dtype, down = {"e4m3": (ml_dtypes.float8_e4m3fn, 7), "e5m2": (ml_dtypes.float8_e5m2, 14)}[fmt]
    v = np.moveaxis(np.asarray(x, np.float32).astype(ml_dtypes.bfloat16).astype(np.float64), axis, -1)
    blocks = v.reshape(v.shape[:-1] + (-1, 32))
    amax = np.abs(blocks).max(-1, keepdims=True)
    byte = np.maximum(np.where(amax > 0, np.frexp(amax)[1] - 1 + 127, 0) - down, 1)
    scale = np.exp2(byte - 127.0)
    codes = (blocks / scale).astype(np.float32).astype(dtype).astype(np.float64)
    return np.moveaxis((codes * scale).reshape(v.shape), -1, axis)


WIDE = False


def mx_kscale(k):
    if not WIDE:
        return np.ones(k)
    levels = np.array([10, -10, 5, -5, 0])
    if k % 512:
        return np.exp2(np.random.permutation(np.resize(levels, k // 32))).repeat(32)
    a = np.empty((k // 512, 16))
    for p in range(k // 512):
        a[p, :8] = np.random.permutation(np.resize(levels, 8))
        for g in range(8):
            far = levels[np.abs(levels - a[p, g]) >= 10]
            a[p, g + 8] = far[np.random.randint(len(far))]
    return np.exp2(a.ravel()).repeat(32)


def f64(x):
    return np.asarray(x).astype(np.float64)


def striped(idx):
    return np.tile(idx.reshape(-1, 16).T, (8, 1)).astype(np.uint16)


def unstriped(offs):
    return offs[:16].T.reshape(-1).astype(np.int64)


def gelu(v):
    return 0.5 * v * (1.0 + np.tanh(np.sqrt(2.0 / np.pi) * (v + 0.044715 * v**3)))


K, T, E, C, H, N = 512, 1536, 8, 128, 512, 128


def by_expert(wq, xq):
    return np.concatenate([wq[e].T @ xq[:, e * C:(e + 1) * C] for e in range(E)], axis=1)


def setup_inputs():
    n = np.random.standard_normal
    s = mx_kscale(K)[:, None]
    u = mx_kscale(H)
    return {
        "xT": (n((K, T)) * s).astype(np.float32),
        "w1": (n((E, K, H)) / np.sqrt(K) / s[None] * u[None, None, :]).astype(np.float32),
        "w2": (n((E, H, N)) / np.sqrt(H) / u[None, :, None]).astype(np.float32),
        "gate": np.tile(np.random.uniform(0.2, 1.0, E * C), (N, 1)).astype(np.float32),
        "offs": striped(np.random.permutation(T)[:E * C]),
        "dst": striped(np.random.permutation(T)[:E * C]),
    }


def reference(xT, w1, w2, gate, offs, dst):
    idx = unstriped(offs)
    xq = mxq(f64(xT)[:, idx], 0, "e4m3")
    h = gelu(by_expert(mxq(f64(w1), 1, "e4m3"), xq))
    y = by_expert(mxq(f64(w2), 1, "e4m3"), mxq(h, 0, "e4m3"))
    out = np.zeros((N, T))
    out[:, unstriped(dst)] = f64(gate) * y
    return out

@@ -1,0 +1,170 @@
+from contextlib import ExitStack
+
+import concourse.mybir as mybir
+
+F32 = mybir.dt.float32
+BF16 = mybir.dt.bfloat16
+U32 = mybir.dt.uint32
+U16 = mybir.dt.uint16
+U8 = mybir.dt.uint8
+X4 = mybir.dt.float8_e4m3fn_x4
+GELU = mybir.ActivationFunctionType.Gelu_apprx_tanh
+COPY = mybir.ActivationFunctionType.Copy
+MULT = mybir.AluOpType.mult
+
+P = 128
+K, T, E, C, H, N = 512, 1536, 8, 128, 512, 128
+S = E * C
+FLOPS = 2 * S * K * H + 2 * S * H * N
+
+CFG = {"x":[0,256,512,1024,1536],"xf":[0.625,0.625,0.625,0.625],"loads":["x0","x1","offs","x2","x3","w0","u0","w1","g0","w2","u1","w3","w4","u2","w5","w6","w7","u3","g1"],"gath":[[0,256],[256,256],[512,512]],"gdep":{},"mv":[64,64,64,64,64,64,64,64],"uv":[0,0,0,0],"lag":{"0":1,"1":2,"2":3,"3":4,"4":5,"5":6,"6":7},"ylag":{"0":1,"1":2,"2":3},"text":["x0","x1","x2","x3","G0","w0","u0","m0","G1","w1","m1","h0","w2","u1","m2","h1","G2","w3","m3","h2","y0","w4","u2","m4","h3","w5","m5","h4","y1","w6","u3","m6","h5","w7","m7","h6","y2","h7","y3"]}
+
+
+def tile_moe_two_mlp_gelu_kernel(tc, xT, w1, w2, gate, offs, dst, out):
+    nc = tc.nc
+    X = CFG["x"]
+    NX = len(X) - 1
+    with ExitStack() as ctx:
+        lists = ctx.enter_context(tc.tile_pool(name="lists", bufs=1))
+        keep = ctx.enter_context(tc.tile_pool(name="keep", bufs=1))
+        psum_a = ctx.enter_context(tc.psum_pool(name="psum_a", bufs=5))
+        psum_y = ctx.enter_context(tc.psum_pool(name="psum_y", bufs=3))
+
+        offs_sb = lists.tile([P, S // 16], U16, name="offs_sb")
+        dst_sb = lists.tile([P, S // 16], U16, name="dst_sb")
+
+        x_raw = [keep.tile([P, 4, X[c + 1] - X[c]], F32, name=f"x_raw{c}") for c in range(NX)]
+        x_bf = [keep.tile([P, X[c + 1] - X[c], 4], BF16, name=f"x_bf{c}", align_bytes=64) for c in range(NX)]
+        x_codes = keep.tile([P, T], U32, name="x_codes", align_bytes=64)
+        x_scales = keep.tile([P, T], U8, name="x_scales", align_bytes=64)
+        w1_raw = [keep.tile([P, 4, H], F32, name=f"w1_raw{e}", tag=f"w1_raw{e}", align_bytes=64) for e in range(E)]
+        w1_bf = [keep.tile([P, 4, P, 4], BF16, name=f"w1_bf{e}", align_bytes=64) for e in range(E)]
+        w1_codes = [keep.tile([P, H], U32, name=f"w1_codes{e}", align_bytes=64) for e in range(E)]
+        w1_scales = [keep.tile([P, H], U8, name=f"w1_scales{e}", align_bytes=64) for e in range(E)]
+        w2_raw = [keep.tile([P, 2, 4, N], F32, name=f"w2_raw{q}", tag=f"w2_raw{q}", align_bytes=64) for q in range(E // 2)]
+        w2_bf = [keep.tile([P, 2, N, 4], BF16, name=f"w2_bf{q}", align_bytes=64) for q in range(E // 2)]
+        w2_codes = [keep.tile([P, 2 * N], U32, name=f"w2_codes{q}", align_bytes=64) for q in range(E // 2)]
+        w2_scales = [keep.tile([P, 2 * N], U8, name=f"w2_scales{q}", align_bytes=64) for q in range(E // 2)]
+        h_codes = [keep.tile([P, C], U32, name=f"h_codes{e}", align_bytes=64) for e in range(E)]
+        h_scales = [keep.tile([P, C], U8, name=f"h_scales{e}", align_bytes=64) for e in range(E)]
+        gate_sb = keep.tile([P, S], F32, name="gate_sb")
+        out_sb = keep.tile([P, T], F32, name="out_sb")
+        warm = keep.tile([P, 2], F32, name="warm")
+
+        x_rows = xT.rearrange("(p j) c -> p j c", j=4)
+        for ld in CFG["loads"]:
+            if ld == "offs":
+                nc.sync.dma_start(offs_sb[:], offs)
+                nc.sync.dma_start(dst_sb[:], dst)
+                continue
+            k = int(ld[1:])
+            if ld[0] == "x":
+                nc.sync.dma_start(x_raw[k][:], x_rows[:, :, X[k] : X[k + 1]])
+            if ld[0] == "w":
+                nc.sync.dma_start(w1_raw[k][:], w1[k].rearrange("(p j) i -> p j i", j=4))
+            if ld[0] == "u":
+                nc.sync.dma_start(w2_raw[k][:], w2[2 * k : 2 * k + 2].rearrange("e (p t) n -> p e t n", t=4))
+            if ld[0] == "g":
+                h0 = k * S // 2
+                nc.sync.dma_start(gate_sb[:, h0 : h0 + S // 2], gate[:, h0 : h0 + S // 2])
+
+        nc.vector.memset(warm[:], 0.0)
+        nc.scalar.activation(warm[:, 1:2], warm[:, 0:1], GELU)
+        nc.gpsimd.memset(x_scales[:], 0)
+        nc.gpsimd.memset(out_sb[:], 0.0)
+
+        def move(on_scalar, to, frm):
+            if on_scalar:
+                nc.scalar.activation(to, frm, COPY)
+            else:
+                nc.vector.tensor_copy(to, frm)
+
+        def x_copy(c, lo, hi, on_scalar):
+            if lo < hi:
+                move(on_scalar, x_bf[c][:, lo:hi, :].rearrange("p (c i) j -> p c j i", i=4),
+                     x_raw[c][:, :, lo:hi].rearrange("p j (c i) -> p c j i", i=4))
+
+        def quantize(codes, scales, values):
+            nc.vector.quantize_mx(out=codes.bitcast(X4), scales=scales, in_=values)
+
+        def w1_copy(e, m0, m1, on_scalar):
+            if m0 < m1:
+                move(on_scalar, w1_bf[e][:, :, m0:m1, :].rearrange("p t m j -> p m j t"),
+                     w1_raw[e][:, :, 4 * m0 : 4 * m1].rearrange("p j (m t) -> p m j t", t=4))
+
+        acc = {}
+        y_acc = {}
+        s_codes = {}
+        s_scales = {}
+
+        def do_x(c):
+            w = X[c + 1] - X[c]
+            cut = int(w * CFG["xf"][c]) // 8 * 8
+            x_copy(c, 0, cut, False)
+            x_copy(c, cut, w, True)
+            quantize(x_codes[:, X[c] : X[c + 1]], x_scales[:, X[c] : X[c + 1]], x_bf[c][:].rearrange("p c j -> p (c j)"))
+
+        def do_g(i):
+            a, n = CFG["gath"][i]
+            lst = offs_sb[:, a // 16 : (a + n) // 16]
+            tags = [f"w1_raw{CFG['gdep'][str(i) + s]}" if str(i) + s in CFG["gdep"] else f"g{s}{i}" for s in "sc"]
+            s_scales[i] = keep.tile([P, n], U8, name=f"s_scales{i}", tag=tags[0], align_bytes=64)
+            s_codes[i] = keep.tile([P, n], U32, name=f"s_codes{i}", tag=tags[1], align_bytes=64)
+            nc.vector.tensor_copy(s_scales[i][:], x_scales[:].indirect(lst))
+            nc.vector.tensor_copy(s_codes[i][:], x_codes[:].indirect(lst))
+
+        def do_w(e):
+            m = CFG["mv"][e]
+            w1_copy(e, 0, m, False)
+            w1_copy(e, m, P, True)
+            quantize(w1_codes[e][:], w1_scales[e][:], w1_bf[e][:].rearrange("p t m j -> p (t m j)"))
+
+        def do_u(q):
+            for u in range(2):
+                move(not CFG["uv"][q], w2_bf[q][:, u, :, :].rearrange("p (c i) t -> p c t i", i=4),
+                     w2_raw[q][:, u, :, :].rearrange("p t (c i) -> p c t i", i=4))
+            quantize(w2_codes[q][:], w2_scales[q][:], w2_bf[q][:].rearrange("p u n t -> p (u n t)"))
+
+        def do_m(e):
+            i, a = [(i, e * C - a) for i, (a, n) in enumerate(CFG["gath"]) if a <= e * C < a + n][0]
+            acc[e] = psum_a.tile([P, 4, C], F32, name="acc")
+            for t in range(4):
+                nc.tensor.matmul_mx(
+                    out=acc[e][:, t, :],
+                    lhsT=w1_codes[e][:, t * P : (t + 1) * P].bitcast(X4),
+                    lhsT_scale=w1_scales[e][:, t * P : (t + 1) * P],
+                    rhs=s_codes[i][:, a : a + C].bitcast(X4),
+                    rhs_scale=s_scales[i][:, a : a + C],
+                    start=True,
+                    stop=True,
+                )
+
+        def do_h(e):
+            q, u = e // 2, e % 2
+            tag = f"w1_raw{CFG['lag'][str(e)]}" if str(e) in CFG["lag"] else f"h_bf{e}"
+            h_bf = keep.tile([P, C, 4], BF16, name=f"h_bf{e}", tag=tag, align_bytes=64)
+            nc.scalar.activation(h_bf[:], acc[e][:].rearrange("p t n -> p n t"), GELU)
+            quantize(h_codes[e][:], h_scales[e][:], h_bf[:].rearrange("p n t -> p (n t)"))
+            if q not in y_acc:
+                y_acc[q] = psum_y.tile([P, 2 * C], F32, name="y_acc")
+            nc.tensor.matmul_mx(
+                out=y_acc[q][:, u * C : (u + 1) * C],
+                lhsT=w2_codes[q][:, u * N : (u + 1) * N].bitcast(X4),
+                lhsT_scale=w2_scales[q][:, u * N : (u + 1) * N],
+                rhs=h_codes[e][:].bitcast(X4),
+                rhs_scale=h_scales[e][:],
+                start=True,
+                stop=True,
+            )
+
+        def do_y(q):
+            tag = f"w2_raw{CFG['ylag'][str(q)]}" if str(q) in CFG["ylag"] else f"y_sb{q}"
+            y_sb = keep.tile([P, 2 * C], F32, name=f"y_sb{q}", tag=tag, align_bytes=64)
+            nc.scalar.copy(y_sb[:], y_acc[q][:])
+            a = 2 * C * q
+            nc.vector.tensor_tensor(out_sb[:].indirect(dst_sb[:, a // 16 : a // 16 + 16]), y_sb[:], gate_sb[:, a : a + 2 * C], MULT)
+
+        steps = {"x": do_x, "G": do_g, "w": do_w, "u": do_u, "m": do_m, "h": do_h, "y": do_y}
+        for item in CFG["text"]:
+            steps[item[0]](int(item[1:]))
+        nc.sync.dma_start(out, out_sb[:])

@@ -17,7 +17,7 @@ K, T, E, C, H, N = 512, 1536, 8, 128, 512, 128
 S = E * C
 FLOPS = 2 * S * K * H + 2 * S * H * N
 
-CFG = {"x":[0,256,512,1024,1536],"xf":[0.625,0.625,0.625,0.625],"loads":["x0","x1","offs","x2","x3","w0","u0","w1","g0","w2","u1","w3","w4","u2","w5","w6","w7","u3","g1"],"gath":[[0,256],[256,256],[512,512]],"gdep":{},"mv":[64,64,64,64,64,64,64,64],"uv":[0,0,0,0],"lag":{"0":1,"1":2,"2":3,"3":4,"4":5,"5":6,"6":7},"ylag":{"0":1,"1":2,"2":3},"text":["x0","x1","x2","x3","G0","w0","u0","m0","G1","w1","m1","h0","w2","u1","m2","h1","G2","w3","m3","h2","y0","w4","u2","m4","h3","w5","m5","h4","y1","w6","u3","m6","h5","w7","m7","h6","y2","h7","y3"]}
+CFG = {"x":[0,512,1024,1280,1536],"xf":[0.625,0.625,0.375,0.5],"loads":["x0","x1","x2","offs","x3","w0","w1","u0","w2","w3","u1","g0","w4","w5","u2","w6","w7","u3","g1"],"gath":[[0,256],[256,768]],"gdep":{"1s":0},"mv":[0,16,64,128,32,128,16,96],"uv":[0,0,0,0],"lag":{"0":1,"1":2,"2":3,"3":4,"4":5,"5":6,"6":7},"ylag":{"0":1,"1":2},"ys":[[0,256],[256,256],[512,256],[768,128],[896,128]],"scat":[[0,256],[256,256],[512,256],[768,256]],"text":["x0","x1","x2","x3","G0","w0","u0","m0","G1","w1","m1","h0","w2","u1","m2","h1","w3","m3","h2","y0","k0","w4","u2","m4","h3","w5","m5","h4","y1","k1","w6","u3","m6","h5","w7","m7","h6","y2","k2","h7","y3","y4","k3"],"comps":[[0,256],[256,512],[512,768],[768,1024]]}
 
 
 def tile_moe_two_mlp_gelu_kernel(tc, xT, w1, w2, gate, offs, dst, out):
@@ -120,9 +120,13 @@ def tile_moe_two_mlp_gelu_kernel(tc, xT, w1, w2, gate, offs, dst, out):
             quantize(w1_codes[e][:], w1_scales[e][:], w1_bf[e][:].rearrange("p t m j -> p (t m j)"))
 
         def do_u(q):
-            for u in range(2):
-                move(not CFG["uv"][q], w2_bf[q][:, u, :, :].rearrange("p (c i) t -> p c t i", i=4),
-                     w2_raw[q][:, u, :, :].rearrange("p t (c i) -> p c t i", i=4))
+            if CFG["uv"][q]:
+                nc.vector.tensor_copy(w2_bf[q][:].rearrange("p u (c i) t -> p u c t i", i=4),
+                                      w2_raw[q][:].rearrange("p u t (c i) -> p u c t i", i=4))
+            else:
+                for u in range(2):
+                    nc.scalar.activation(w2_bf[q][:, u, :, :].rearrange("p (c i) t -> p c t i", i=4),
+                                         w2_raw[q][:, u, :, :].rearrange("p t (c i) -> p c t i", i=4), COPY)
             quantize(w2_codes[q][:], w2_scales[q][:], w2_bf[q][:].rearrange("p u n t -> p (u n t)"))
 
         def do_m(e):
@@ -157,14 +161,24 @@ def tile_moe_two_mlp_gelu_kernel(tc, xT, w1, w2, gate, offs, dst, out):
                 stop=True,
             )
 
-        def do_y(q):
-            tag = f"w2_raw{CFG['ylag'][str(q)]}" if str(q) in CFG["ylag"] else f"y_sb{q}"
-            y_sb = keep.tile([P, 2 * C], F32, name=f"y_sb{q}", tag=tag, align_bytes=64)
-            nc.scalar.copy(y_sb[:], y_acc[q][:])
-            a = 2 * C * q
-            nc.vector.tensor_tensor(out_sb[:].indirect(dst_sb[:, a // 16 : a // 16 + 16]), y_sb[:], gate_sb[:, a : a + 2 * C], MULT)
+        y_sb = {}
 
-        steps = {"x": do_x, "G": do_g, "w": do_w, "u": do_u, "m": do_m, "h": do_h, "y": do_y}
+        def do_y(i):
+            a, n = CFG["ys"][i]
+            k, lo, hi = [(k, lo, hi) for k, (lo, hi) in enumerate(CFG["comps"]) if lo <= a < hi][0]
+            if k not in y_sb:
+                tag = f"w2_raw{CFG['ylag'][str(k)]}" if str(k) in CFG["ylag"] else f"y_sb{k}"
+                y_sb[k] = keep.tile([P, hi - lo], F32, name=f"y_sb{k}", tag=tag, align_bytes=64)
+            nc.scalar.copy(y_sb[k][:, a - lo : a - lo + n], y_acc[a // (2 * C)][:, a % (2 * C) : a % (2 * C) + n])
+
+        def do_k(i):
+            a, n = CFG["scat"][i]
+            k, lo = [(k, lo) for k, (lo, hi) in enumerate(CFG["comps"]) if lo <= a < hi][0]
+            nc.vector.tensor_tensor(
+                out_sb[:].indirect(dst_sb[:, a // 16 : (a + n) // 16]), y_sb[k][:, a - lo : a - lo + n], gate_sb[:, a : a + n], MULT
+            )
+
+        steps = {"x": do_x, "G": do_g, "w": do_w, "u": do_u, "m": do_m, "h": do_h, "y": do_y, "k": do_k}
         for item in CFG["text"]:
             steps[item[0]](int(item[1:]))
         nc.sync.dma_start(out, out_sb[:])

@@ -17,7 +17,7 @@ K, T, E, C, H, N = 512, 1536, 8, 128, 512, 128
 S = E * C
 FLOPS = 2 * S * K * H + 2 * S * H * N
 
-CFG = {"x":[0,512,1024,1280,1536],"xf":[0.625,0.625,0.375,0.5],"loads":["x0","x1","x2","offs","x3","w0","w1","u0","w2","w3","u1","g0","w4","w5","u2","w6","w7","u3","g1"],"gath":[[0,256],[256,768]],"gdep":{"1s":0},"mv":[0,16,64,128,32,128,16,96],"uv":[0,0,0,0],"lag":{"0":1,"1":2,"2":3,"3":4,"4":5,"5":6,"6":7},"ylag":{"0":1,"1":2},"ys":[[0,256],[256,256],[512,256],[768,128],[896,128]],"scat":[[0,256],[256,256],[512,256],[768,256]],"text":["x0","x1","x2","x3","G0","w0","u0","m0","G1","w1","m1","h0","w2","u1","m2","h1","w3","m3","h2","y0","k0","w4","u2","m4","h3","w5","m5","h4","y1","k1","w6","u3","m6","h5","w7","m7","h6","y2","k2","h7","y3","y4","k3"],"comps":[[0,256],[256,512],[512,768],[768,1024]]}
+CFG = {"x":[0,256,768,1280,1536],"xf":[0.625,0.875,0.625,0.25],"loads":["x0","x1","x2","offs","x3","w0","w1","w2","u0","w3","u1","g0","w4","w5","w6","u2","w7","u3","g1"],"gath":[[0,512],[512,512]],"gdep":{"1s":0},"mv":[0,0,48,16,16,64,16,16],"uv":[1,1,1,1],"lag":{"2":3,"3":4,"5":6,"6":7},"ylag":{"0":1,"2":3},"ys":[[0,256],[256,256],[512,256],[768,128],[896,128]],"scat":[[0,256],[256,256],[512,256],[768,256]],"text":["x0","x1","x2","x3","G0","w0","m0","w1","u0","m1","h0","w2","m2","h1","w3","u1","m3","G1","h2","y0","k0","w4","m4","h3","w5","u2","m5","h4","y1","k1","w6","m6","h5","w7","u3","m7","h6","y2","k2","h7","y3","y4","k3"],"comps":[[0,256],[256,512],[512,768],[768,1024]]}
 
 
 def tile_moe_two_mlp_gelu_kernel(tc, xT, w1, w2, gate, offs, dst, out):

from contextlib import ExitStack

import concourse.mybir as mybir

F32 = mybir.dt.float32
BF16 = mybir.dt.bfloat16
U32 = mybir.dt.uint32
U16 = mybir.dt.uint16
U8 = mybir.dt.uint8
X4 = mybir.dt.float8_e4m3fn_x4
GELU = mybir.ActivationFunctionType.Gelu_apprx_tanh
COPY = mybir.ActivationFunctionType.Copy
MULT = mybir.AluOpType.mult

P = 128
K, T, E, C, H, N = 512, 1536, 8, 128, 512, 128
S = E * C
FLOPS = 2 * S * K * H + 2 * S * H * N

CFG = {"x":[0,256,768,1280,1536],"xf":[0.625,0.875,0.625,0.25],"loads":["x0","x1","x2","offs","x3","w0","w1","w2","u0","w3","u1","g0","w4","w5","w6","u2","w7","u3","g1"],"gath":[[0,512],[512,512]],"gdep":{"1s":0},"mv":[0,0,48,16,16,64,16,16],"uv":[1,1,1,1],"lag":{"2":3,"3":4,"5":6,"6":7},"ylag":{"0":1,"2":3},"ys":[[0,256],[256,256],[512,256],[768,128],[896,128]],"scat":[[0,256],[256,256],[512,256],[768,256]],"text":["x0","x1","x2","x3","G0","w0","m0","w1","u0","m1","h0","w2","m2","h1","w3","u1","m3","G1","h2","y0","k0","w4","m4","h3","w5","u2","m5","h4","y1","k1","w6","m6","h5","w7","u3","m7","h6","y2","k2","h7","y3","y4","k3"],"comps":[[0,256],[256,512],[512,768],[768,1024]]}


def tile_moe_two_mlp_gelu_kernel(tc, xT, w1, w2, gate, offs, dst, out):
    nc = tc.nc
    X = CFG["x"]
    NX = len(X) - 1
    with ExitStack() as ctx:
        lists = ctx.enter_context(tc.tile_pool(name="lists", bufs=1))
        keep = ctx.enter_context(tc.tile_pool(name="keep", bufs=1))
        psum_a = ctx.enter_context(tc.psum_pool(name="psum_a", bufs=5))
        psum_y = ctx.enter_context(tc.psum_pool(name="psum_y", bufs=3))

        offs_sb = lists.tile([P, S // 16], U16, name="offs_sb")
        dst_sb = lists.tile([P, S // 16], U16, name="dst_sb")

        x_raw = [keep.tile([P, 4, X[c + 1] - X[c]], F32, name=f"x_raw{c}") for c in range(NX)]
        x_bf = [keep.tile([P, X[c + 1] - X[c], 4], BF16, name=f"x_bf{c}", align_bytes=64) for c in range(NX)]
        x_codes = keep.tile([P, T], U32, name="x_codes", align_bytes=64)
        x_scales = keep.tile([P, T], U8, name="x_scales", align_bytes=64)
        w1_raw = [keep.tile([P, 4, H], F32, name=f"w1_raw{e}", tag=f"w1_raw{e}", align_bytes=64) for e in range(E)]
        w1_bf = [keep.tile([P, 4, P, 4], BF16, name=f"w1_bf{e}", align_bytes=64) for e in range(E)]
        w1_codes = [keep.tile([P, H], U32, name=f"w1_codes{e}", align_bytes=64) for e in range(E)]
        w1_scales = [keep.tile([P, H], U8, name=f"w1_scales{e}", align_bytes=64) for e in range(E)]
        w2_raw = [keep.tile([P, 2, 4, N], F32, name=f"w2_raw{q}", tag=f"w2_raw{q}", align_bytes=64) for q in range(E // 2)]
        w2_bf = [keep.tile([P, 2, N, 4], BF16, name=f"w2_bf{q}", align_bytes=64) for q in range(E // 2)]
        w2_codes = [keep.tile([P, 2 * N], U32, name=f"w2_codes{q}", align_bytes=64) for q in range(E // 2)]
        w2_scales = [keep.tile([P, 2 * N], U8, name=f"w2_scales{q}", align_bytes=64) for q in range(E // 2)]
        h_codes = [keep.tile([P, C], U32, name=f"h_codes{e}", align_bytes=64) for e in range(E)]
        h_scales = [keep.tile([P, C], U8, name=f"h_scales{e}", align_bytes=64) for e in range(E)]
        gate_sb = keep.tile([P, S], F32, name="gate_sb")
        out_sb = keep.tile([P, T], F32, name="out_sb")
        warm = keep.tile([P, 2], F32, name="warm")

        x_rows = xT.rearrange("(p j) c -> p j c", j=4)
        for ld in CFG["loads"]:
            if ld == "offs":
                nc.sync.dma_start(offs_sb[:], offs)
                nc.sync.dma_start(dst_sb[:], dst)
                continue
            k = int(ld[1:])
            if ld[0] == "x":
                nc.sync.dma_start(x_raw[k][:], x_rows[:, :, X[k] : X[k + 1]])
            if ld[0] == "w":
                nc.sync.dma_start(w1_raw[k][:], w1[k].rearrange("(p j) i -> p j i", j=4))
            if ld[0] == "u":
                nc.sync.dma_start(w2_raw[k][:], w2[2 * k : 2 * k + 2].rearrange("e (p t) n -> p e t n", t=4))
            if ld[0] == "g":
                h0 = k * S // 2
                nc.sync.dma_start(gate_sb[:, h0 : h0 + S // 2], gate[:, h0 : h0 + S // 2])

        nc.vector.memset(warm[:], 0.0)
        nc.scalar.activation(warm[:, 1:2], warm[:, 0:1], GELU)
        nc.gpsimd.memset(x_scales[:], 0)
        nc.gpsimd.memset(out_sb[:], 0.0)

        def move(on_scalar, to, frm):
            if on_scalar:
                nc.scalar.activation(to, frm, COPY)
            else:
                nc.vector.tensor_copy(to, frm)

        def x_copy(c, lo, hi, on_scalar):
            if lo < hi:
                move(on_scalar, x_bf[c][:, lo:hi, :].rearrange("p (c i) j -> p c j i", i=4),
                     x_raw[c][:, :, lo:hi].rearrange("p j (c i) -> p c j i", i=4))

        def quantize(codes, scales, values):
            nc.vector.quantize_mx(out=codes.bitcast(X4), scales=scales, in_=values)

        def w1_copy(e, m0, m1, on_scalar):
            if m0 < m1:
                move(on_scalar, w1_bf[e][:, :, m0:m1, :].rearrange("p t m j -> p m j t"),
                     w1_raw[e][:, :, 4 * m0 : 4 * m1].rearrange("p j (m t) -> p m j t", t=4))

        acc = {}
        y_acc = {}
        s_codes = {}
        s_scales = {}

        def do_x(c):
            w = X[c + 1] - X[c]
            cut = int(w * CFG["xf"][c]) // 8 * 8
            x_copy(c, 0, cut, False)
            x_copy(c, cut, w, True)
            quantize(x_codes[:, X[c] : X[c + 1]], x_scales[:, X[c] : X[c + 1]], x_bf[c][:].rearrange("p c j -> p (c j)"))

        def do_g(i):
            a, n = CFG["gath"][i]
            lst = offs_sb[:, a // 16 : (a + n) // 16]
            tags = [f"w1_raw{CFG['gdep'][str(i) + s]}" if str(i) + s in CFG["gdep"] else f"g{s}{i}" for s in "sc"]
            s_scales[i] = keep.tile([P, n], U8, name=f"s_scales{i}", tag=tags[0], align_bytes=64)
            s_codes[i] = keep.tile([P, n], U32, name=f"s_codes{i}", tag=tags[1], align_bytes=64)
            nc.vector.tensor_copy(s_scales[i][:], x_scales[:].indirect(lst))
            nc.vector.tensor_copy(s_codes[i][:], x_codes[:].indirect(lst))

        def do_w(e):
            m = CFG["mv"][e]
            w1_copy(e, 0, m, False)
            w1_copy(e, m, P, True)
            quantize(w1_codes[e][:], w1_scales[e][:], w1_bf[e][:].rearrange("p t m j -> p (t m j)"))

        def do_u(q):
            if CFG["uv"][q]:
                nc.vector.tensor_copy(w2_bf[q][:].rearrange("p u (c i) t -> p u c t i", i=4),
                                      w2_raw[q][:].rearrange("p u t (c i) -> p u c t i", i=4))
            else:
                for u in range(2):
                    nc.scalar.activation(w2_bf[q][:, u, :, :].rearrange("p (c i) t -> p c t i", i=4),
                                         w2_raw[q][:, u, :, :].rearrange("p t (c i) -> p c t i", i=4), COPY)
            quantize(w2_codes[q][:], w2_scales[q][:], w2_bf[q][:].rearrange("p u n t -> p (u n t)"))

        def do_m(e):
            i, a = [(i, e * C - a) for i, (a, n) in enumerate(CFG["gath"]) if a <= e * C < a + n][0]
            acc[e] = psum_a.tile([P, 4, C], F32, name="acc")
            for t in range(4):
                nc.tensor.matmul_mx(
                    out=acc[e][:, t, :],
                    lhsT=w1_codes[e][:, t * P : (t + 1) * P].bitcast(X4),
                    lhsT_scale=w1_scales[e][:, t * P : (t + 1) * P],
                    rhs=s_codes[i][:, a : a + C].bitcast(X4),
                    rhs_scale=s_scales[i][:, a : a + C],
                    start=True,
                    stop=True,
                )

        def do_h(e):
            q, u = e // 2, e % 2
            tag = f"w1_raw{CFG['lag'][str(e)]}" if str(e) in CFG["lag"] else f"h_bf{e}"
            h_bf = keep.tile([P, C, 4], BF16, name=f"h_bf{e}", tag=tag, align_bytes=64)
            nc.scalar.activation(h_bf[:], acc[e][:].rearrange("p t n -> p n t"), GELU)
            quantize(h_codes[e][:], h_scales[e][:], h_bf[:].rearrange("p n t -> p (n t)"))
            if q not in y_acc:
                y_acc[q] = psum_y.tile([P, 2 * C], F32, name="y_acc")
            nc.tensor.matmul_mx(
                out=y_acc[q][:, u * C : (u + 1) * C],
                lhsT=w2_codes[q][:, u * N : (u + 1) * N].bitcast(X4),
                lhsT_scale=w2_scales[q][:, u * N : (u + 1) * N],
                rhs=h_codes[e][:].bitcast(X4),
                rhs_scale=h_scales[e][:],
                start=True,
                stop=True,
            )

        y_sb = {}

        def do_y(i):
            a, n = CFG["ys"][i]
            k, lo, hi = [(k, lo, hi) for k, (lo, hi) in enumerate(CFG["comps"]) if lo <= a < hi][0]
            if k not in y_sb:
                tag = f"w2_raw{CFG['ylag'][str(k)]}" if str(k) in CFG["ylag"] else f"y_sb{k}"
                y_sb[k] = keep.tile([P, hi - lo], F32, name=f"y_sb{k}", tag=tag, align_bytes=64)
            nc.scalar.copy(y_sb[k][:, a - lo : a - lo + n], y_acc[a // (2 * C)][:, a % (2 * C) : a % (2 * C) + n])

        def do_k(i):
            a, n = CFG["scat"][i]
            k, lo = [(k, lo) for k, (lo, hi) in enumerate(CFG["comps"]) if lo <= a < hi][0]
            nc.vector.tensor_tensor(
                out_sb[:].indirect(dst_sb[:, a // 16 : (a + n) // 16]), y_sb[k][:, a - lo : a - lo + n], gate_sb[:, a : a + n], MULT
            )

        steps = {"x": do_x, "G": do_g, "w": do_w, "u": do_u, "m": do_m, "h": do_h, "y": do_y, "k": do_k}
        for item in CFG["text"]:
            steps[item[0]](int(item[1:]))
        nc.sync.dma_start(out, out_sb[:])
